import numpy as np
import ml_dtypes


def mxq(x, axis, fmt="e4m3"):
    dtype, down = {"e4m3": (ml_dtypes.float8_e4m3fn, 7), "e5m2": (ml_dtypes.float8_e5m2, 14)}[fmt]
    v = np.moveaxis(np.asarray(x, np.float32).astype(ml_dtypes.bfloat16).astype(np.float64), axis, -1)
    blocks = v.reshape(v.shape[:-1] + (-1, 32))
    amax = np.abs(blocks).max(-1, keepdims=True)
    byte = np.maximum(np.where(amax > 0, np.frexp(amax)[1] - 1 + 127, 0) - down, 1)
    scale = np.exp2(byte - 127.0)
    codes = (blocks / scale).astype(np.float32).astype(dtype).astype(np.float64)
    return np.moveaxis((codes * scale).reshape(v.shape), -1, axis)


WIDE = False


def mx_kscale(k):
    if not WIDE:
        return np.ones(k)
    levels = np.array([10, -10, 5, -5, 0])
    if k % 512:
        return np.exp2(np.random.permutation(np.resize(levels, k // 32))).repeat(32)
    a = np.empty((k // 512, 16))
    for p in range(k // 512):
        a[p, :8] = np.random.permutation(np.resize(levels, 8))
        for g in range(8):
            far = levels[np.abs(levels - a[p, g]) >= 10]
            a[p, g + 8] = far[np.random.randint(len(far))]
    return np.exp2(a.ravel()).repeat(32)


def f64(x):
    return np.asarray(x).astype(np.float64)


def striped(idx):
    return np.tile(idx.reshape(-1, 16).T, (8, 1)).astype(np.uint16)


def unstriped(offs):
    return offs[:16].T.reshape(-1).astype(np.int64)


def striped8(idx):
    return np.concatenate([x.reshape(-1, 16).T for x in idx]).astype(np.uint16)


def runs(offs, k):
    lists = np.stack([offs[16 * r : 16 * r + 16].T.reshape(-1) for r in range(8)]).astype(np.int64)
    return lists[np.arange(k) % 512 // 64]


def pack_weight(w):
    k, n = w.shape
    w = f64(np.asarray(w, np.float32).astype(ml_dtypes.bfloat16)).reshape(k // 32, 32, n)
    amax = np.abs(w).max(1)
    byte = np.clip(np.where(amax > 0, np.frexp(amax)[1] - 1 + 127 - 7, 1), 1, 254)
    scaled = (w * np.exp2(127.0 - byte)[:, None, :]).reshape(k, n).astype(np.float32)
    words = np.ascontiguousarray(scaled.reshape(k // 512, 128, 4, n).transpose(0, 1, 3, 2)).astype(ml_dtypes.float8_e4m3fn).view(np.uint8)
    return words, np.ascontiguousarray(byte.astype(np.uint8).reshape(k // 512, 16, n))


def unpack_weight(words, scales):
    g, p, n, _ = words.shape
    vals = np.ascontiguousarray(words).view(ml_dtypes.float8_e4m3fn).astype(np.float64) * np.repeat(np.exp2(scales.astype(np.float64) - 127.0), 8, axis=1)[..., None]
    return vals.transpose(0, 1, 3, 2).reshape(g * 512, n)


def relu(v):
    return np.maximum(v, 0.0)

def planes(y):
    n, m = y.shape
    v = y.astype(np.float32).astype(ml_dtypes.bfloat16).astype(np.float64).reshape(n // 32, 32, m)
    top = np.abs(v).max(1)
    byte = np.clip(np.where(top > 0, np.frexp(top)[1] - 1 + 127 - 7, 1), 1, 254)
    codes = (v * np.exp2(127.0 - byte)[:, None, :]).reshape(n, m).astype(np.float32).astype(ml_dtypes.float8_e4m3fn).view(np.uint8)
    words = codes.reshape(n // 512, 128, 4, m).transpose(0, 1, 3, 2)
    return np.ascontiguousarray(words), np.ascontiguousarray(byte.astype(np.uint8).reshape(n // 512, 16, m))


K, T, S, G, H, C = 512, 1024, 512, 2048, 512, 512


def setup_inputs():
    n = np.random.standard_normal
    s = mx_kscale(K)[:, None]
    packed_xT = pack_weight(n((K, T)) * s)
    packed_dT = pack_weight(n((K, G)) / s)
    return {
        "x_words": packed_xT[0],
        "x_scales": packed_xT[1],
        "d_words": packed_dT[0],
        "d_scales": packed_dT[1],
        "gs": (np.random.uniform(0.5, 1.5, (K, 1)) / s).astype(np.float32),
        "offs": striped(np.random.permutation(T)[:S]),
        "k1": striped8(np.random.randint(0, G, (8, H))),
        "n1": striped8(np.stack([np.random.permutation(S) for _ in range(8)])),
        "n2": striped8(np.stack([np.random.permutation(S) for _ in range(8)])),
        "n3": striped8(np.stack([np.random.permutation(S) for _ in range(8)])),
        "cand": striped(np.random.permutation(T)[:C]),
        "n4": striped8(np.stack([np.random.permutation(S) for _ in range(8)])),
    }


def reference(x_words, x_scales, d_words, d_scales, gs, offs, k1, n1, n2, n3, cand, n4):
    x_cand = unpack_weight(x_words, x_scales)[:, unstriped(cand)]
    d_k1 = unpack_weight(d_words, d_scales)[np.arange(K)[:, None], runs(k1, K)]
    xq = unpack_weight(x_words, x_scales)[:, unstriped(offs)]
    h = 0.0625 * (d_k1.T @ xq)
    z = f64(gs) * (0.75 * (h * (h[np.arange(H)[:, None], runs(n1, H)]) + (h[np.arange(H)[:, None], runs(n2, H)]) * (h[np.arange(H)[:, None], runs(n3, H)])))
    s = 0.0625 * ((x_cand.T @ mxq(z, 0, "e4m3")))
    rl = relu(s)
    ds = np.zeros((C, S))
    ds[np.arange(C)[:, None], runs(n4, C)] = rl
    out_0 = ds - (0.5 * s)
    return (out_0,) + planes(out_0)

@@ -1,0 +1,233 @@
+from contextlib import ExitStack
+
+import concourse.mybir as mybir
+from concourse.masks import make_identity
+
+K, T, S, G, H, C = 512, 1024, 512, 2048, 512, 512
+FLOPS = 2 * K * H * S + 2 * K * C * S
+
+F32 = mybir.dt.float32
+BF16 = mybir.dt.bfloat16
+I32 = mybir.dt.int32
+U32 = mybir.dt.uint32
+U16 = mybir.dt.uint16
+U8 = mybir.dt.uint8
+FP8X4 = mybir.dt.float8_e4m3fn_x4
+ALU = mybir.AluOpType
+ACT = mybir.ActivationFunctionType
+
+P = 128
+PACK = 4
+HALF = S // 2
+LIST_COLS = HALF // 16
+
+
+def tile_picked_pqcdotsend_none_po_kernel(
+    tc, x_words, x_scales, d_words, d_scales, gs, offs, k1, n1, n2, n3, cand, n4, out_0, out_1, out_2
+):
+    nc = tc.nc
+    with ExitStack() as ctx:
+        keep = ctx.enter_context(tc.tile_pool(name="keep", bufs=1))
+        reuse = ctx.enter_context(tc.tile_pool(name="reuse", bufs=1))
+        psum = ctx.enter_context(tc.psum_pool(name="psum", bufs=1))
+
+        def load_list(src, name):
+            tile = keep.tile([P, S // 16], U16, name=name)
+            nc.sync.dma_start(tile[:], src)
+            return tile
+
+        def as_words(src):
+            return src[0].rearrange("p n t -> p (n t)").bitcast(I32)
+
+        d_sc = keep.tile([P, G], U8, name="d_sc", align_bytes=64)
+        x_sc = keep.tile([P, T], U8, name="x_sc", align_bytes=64)
+        nc.gpsimd.memset(d_sc[:].bitcast(I32), 0)
+        nc.vector.memset(x_sc[:].bitcast(I32), 0)
+
+        offs_t = load_list(offs, "offs_t")
+        x_w = keep.tile([P, T], U32, name="x_w", align_bytes=64)
+        nc.sync.dma_start(x_w[:].bitcast(I32), as_words(x_words))
+        nc.scalar.dma_start(d_sc[:].bitcast(I32)[0:P:8, :], d_scales[0].bitcast(I32))
+        k1_t = load_list(k1, "k1_t")
+        cand_t = load_list(cand, "cand_t")
+        d_w = keep.tile([P, G], U32, name="d_w", align_bytes=64)
+        nc.sync.dma_start(d_w[:].bitcast(I32), as_words(d_words))
+        for q in range(4):
+            nc.scalar.dma_start(
+                x_sc[:].bitcast(I32)[32 * q : 32 * q + 4, :], x_scales[0].bitcast(I32)[4 * q : 4 * q + 4, :]
+            )
+        gs_t = keep.tile([P, PACK], F32, name="gs_t")
+        nc.sync.dma_start(gs_t[:], gs.rearrange("(p t) o -> p (t o)", t=PACK))
+        n2_t = load_list(n2, "n2_t")
+        n1_t = load_list(n1, "n1_t")
+        n3_t = load_list(n3, "n3_t")
+        n4_t = load_list(n4, "n4_t")
+        ident = keep.tile([P, P], F32, name="ident")
+        make_identity(nc, ident[:])
+
+        gain = keep.tile([P, PACK], F32, name="gain")
+        nc.scalar.activation(gain[:], gs_t[:], ACT.Copy, scale=0.75 * 0.0625)
+
+        def gather(tile, src, lst):
+            nc.vector.tensor_copy(tile[:], src[:].indirect(lst[:]))
+            return tile
+
+        def deal(src, dtype, name):
+            tile = keep.tile([P, S], dtype, name=name, align_bytes=64)
+            nc.vector.tensor_copy(
+                tile[:].rearrange("p (t m) -> p t m", t=PACK), src[:].rearrange("p (m t) -> p t m", t=PACK)
+            )
+            return tile
+
+        xq_w = gather(keep.tile([P, S], U32, name="xq_w", align_bytes=64), x_w, offs_t)
+        dk_sc_raw = gather(keep.tile([P, H], U8, name="dk_sc_raw"), d_sc, k1_t)
+        xc_w_raw = gather(keep.tile([P, C], U32, name="xc_w_raw"), x_w, cand_t)
+        dk_sc = deal(dk_sc_raw, U8, "dk_sc")
+        for c in range(1, 4):
+            queue = nc.scalar if c == 2 else nc.sync
+            queue.dma_start(dk_sc[:].bitcast(I32)[c:P:32, :], dk_sc[:].bitcast(I32)[8 * c : P : 32, :])
+        xc_w = deal(xc_w_raw, U32, "xc_w")
+        dk_w_raw = gather(reuse.tile([P, H], U32, name="dk_w_raw", tag="raw"), d_w, k1_t)
+        xq_sc = gather(keep.tile([P, S], U8, name="xq_sc", align_bytes=64), x_sc, offs_t)
+        dk_w = deal(dk_w_raw, U32, "dk_w")
+
+        h_tiles, a_tiles = [], []
+        for t in range(PACK):
+            cols = slice(P * t, P * (t + 1))
+            acc = psum.tile([P, S], F32, name="h_acc%d" % t, tag="bank%d" % t)
+            nc.tensor.matmul_mx(
+                out=acc[:], lhsT=dk_w[:, cols].bitcast(FP8X4), lhsT_scale=dk_sc[:, cols],
+                rhs=xq_w[:].bitcast(FP8X4), rhs_scale=xq_sc[:], start=True, stop=True,
+            )
+            h_t = keep.tile([P, S], F32, name="h%d" % t)
+            a_t = keep.tile([P, S], F32, name="a%d" % t)
+            nc.scalar.activation(h_t[:], acc[:], ACT.Copy, scale=0.0625)
+            nc.scalar.activation(a_t[:], acc[:], ACT.Copy, scale=gain[:, t : t + 1])
+            h_tiles.append(h_t)
+            a_tiles.append(a_t)
+
+        xc_sc_raw = gather(reuse.tile([P, C], U8, name="xc_sc_raw", tag="raw"), x_sc, cand_t)
+        xc_sc = deal(xc_sc_raw, U8, "xc_sc")
+
+        s_acc = [psum.tile([P, S], F32, name="s_acc%d" % t) for t in range(PACK)]
+        rl = [keep.tile([P, S], F32, name="rl%d" % t) for t in range(PACK)]
+        back = [keep.tile([P, S], F32, name="back%d" % t) for t in range(PACK - 1)]
+
+        def lookups(half, t, sums, h_n2, first):
+            cols = slice(HALF * half, HALF * (half + 1))
+            ent = slice(LIST_COLS * half, LIST_COLS * (half + 1))
+            second = keep.tile([P, HALF], F32, name="second%d_%d" % (half, t))
+            nc.vector.tensor_copy(h_n2, h_tiles[t][:].indirect(n2_t[:, ent]))
+            nc.vector.tensor_tensor(first, h_tiles[t][:].indirect(n1_t[:, ent]), a_tiles[t][:, cols], ALU.mult)
+            nc.vector.tensor_tensor(second[:], a_tiles[t][:].indirect(n3_t[:, ent]), h_n2, ALU.mult)
+            for n, term in enumerate((first, second[:])):
+                for c in range(2):
+                    nc.tensor.matmul(
+                        sums[c][:, P * t : P * (t + 1)], lhsT=term[:, P * c : P * (c + 1)], rhs=ident[:],
+                        is_transpose=True, start=(n == 0), stop=(n == 1),
+                    )
+
+        def half_lookups(half):
+            sums = new_sums(half)
+            first = reuse.tile([P, PACK, HALF], F32, name="first%d" % half, tag="first")
+            for pair in range(2):
+                tag = ("n2_a", "n2_b", "n2_b", "z0")[2 * half + pair]
+                h_n2 = reuse.tile([P, 2, HALF], F32, name="h_n2_%d_%d" % (half, pair), tag=tag, align_bytes=64)
+                for e in range(2):
+                    t = 2 * pair + e
+                    lookups(half, t, sums, h_n2[:, e, :], first[:, t, :])
+            return sums
+
+        def new_sums(half):
+            return [psum.tile([P, S], F32, name="z_t%d_%d" % (half, c), tag="bank%d" % (2 * half + c)) for c in range(2)]
+
+        def score(half, sums):
+            cols = slice(HALF * half, HALF * (half + 1))
+            z_bf = reuse.tile([P, HALF * PACK], BF16, name="z_bf%d" % half, align_bytes=64, tag="z%d" % half)
+            z_bf_words = z_bf[:].bitcast(F32).rearrange("p (j u) -> p j u", u=2)
+            for c in range(2):
+                pairs = psum.tile([P, 2, P], F32, name="pairs%d_%d" % (half, c), tag="bank%d" % (2 - 2 * half + c))
+                z_t = keep.tile([P, 2, P, 2], BF16, name="z_t_bf%d_%d" % (half, c))
+                nc.scalar.copy(z_t[:], sums[c][:].rearrange("j (u e p) -> j u p e", u=2, e=2))
+                z_t_words = z_t[:].rearrange("j u p e -> j (u p e)").bitcast(F32)
+                for u in range(2):
+                    nc.tensor.transpose(pairs[:, u, :], z_t_words[:, P * u : P * (u + 1)], ident[:])
+                nc.scalar.copy(z_bf_words[:, P * c : P * (c + 1), :], pairs[:].rearrange("p u j -> p j u"))
+            z_w = keep.tile([P, HALF], U32, name="z_w%d" % half, align_bytes=64)
+            z_sc = keep.tile([P, HALF], U8, name="z_sc%d" % half, align_bytes=64)
+            nc.vector.quantize_mx(z_w[:].bitcast(FP8X4), z_sc[:], z_bf[:])
+            for t in range(PACK):
+                rows = slice(P * t, P * (t + 1))
+                nc.tensor.matmul_mx(
+                    out=s_acc[t][:, cols], lhsT=xc_w[:, rows].bitcast(FP8X4), lhsT_scale=xc_sc[:, rows],
+                    rhs=z_w[:].bitcast(FP8X4), rhs_scale=z_sc[:], start=True, stop=True,
+                )
+                nc.scalar.activation(rl[t][:, cols], s_acc[t][:, cols], ACT.Relu, scale=0.0625)
+            for t in range(PACK - 1):
+                nc.scalar.activation(back[t][:, cols], s_acc[t][:, cols], ACT.Copy, scale=-0.5 * 0.0625)
+            return z_w
+
+        zw0 = score(0, half_lookups(0))
+        zw1 = score(1, half_lookups(1))
+
+        ds = [
+            keep.tile([P, S], F32, name="ds0"),
+            keep.tile([P, S], F32, name="ds1"),
+            reuse.tile([P, S], F32, name="ds2", tag="z1", align_bytes=64),
+            keep.tile([P, 2 * S], F32, name="ds3"),
+        ]
+        y = keep.tile([P, PACK, S], F32, name="y")
+        y_rows = out_0.rearrange("(p t) j -> p t j", t=PACK)
+
+        def scatter(t, half):
+            nc.vector.tensor_copy(
+                ds[t][:].indirect(n4_t[:, LIST_COLS * half : LIST_COLS * (half + 1)]),
+                rl[t][:, HALF * half : HALF * (half + 1)],
+            )
+
+        def finish_on_tensor(t):
+            y_t = psum.tile([P, S], F32, name="y_t%d" % t, tag="bank%d" % (2 + t % 2))
+            for n, term in enumerate((back[t], ds[t])):
+                for c in range(4):
+                    cols = slice(P * c, P * (c + 1))
+                    nc.tensor.matmul(
+                        y_t[:, cols], lhsT=term[:, cols], rhs=ident[:], is_transpose=True,
+                        start=(n == 0 and c == 0), stop=(n == 1 and c == 3),
+                    )
+            y_t_sb = keep.tile([P, S], F32, name="y_t_sb%d" % t)
+            nc.scalar.copy(y_t_sb[:], y_t[:])
+            y_ps = psum.tile([P, S], F32, name="y_ps%d" % t, tag="bank%d" % (t % 2))
+            for c in range(4):
+                cols = slice(P * c, P * (c + 1))
+                nc.tensor.transpose(y_ps[:, cols], y_t_sb[:, cols], ident[:])
+            nc.scalar.copy(y[:, t, :], y_ps[:])
+            nc.sync.dma_start(y_rows[:, t, :], y[:, t, :])
+
+        for t in range(PACK - 1):
+            scatter(t, 0)
+        for t in range(PACK - 1):
+            scatter(t, 1)
+            finish_on_tensor(t)
+        last = PACK - 1
+        nc.vector.tensor_copy(ds[last][:].indirect(n4_t[:]), rl[last][:])
+        nc.vector.scalar_tensor_tensor(y[:, last, :], s_acc[last][:], -0.5 * 0.0625, ds[last][:, 0:S], ALU.mult, ALU.add)
+        nc.sync.dma_start(y_rows[:, last, :], y[:, last, :])
+
+        y_w = keep.tile([P, S], U32, name="y_w", align_bytes=64)
+        y_sc = keep.tile([P, S], U8, name="y_sc", align_bytes=64)
+        words_out = as_words(out_1)
+        for half in range(2):
+            cols = slice(HALF * half, HALF * (half + 1))
+            y_bf = keep.tile([P, HALF, PACK], BF16, name="y_bf%d" % half, align_bytes=64)
+            dst = y_bf[:].rearrange("p (c i) t -> p c t i", i=4)
+            src = y[:, :, cols].rearrange("p t (c i) -> p c t i", i=4)
+            if half == 0:
+                nc.vector.tensor_copy(dst, src)
+            else:
+                nc.scalar.copy(dst, src)
+            nc.vector.quantize_mx(y_w[:, cols].bitcast(FP8X4), y_sc[:, cols], y_bf[:].rearrange("p j t -> p (j t)"))
+            nc.sync.dma_start(words_out[:, cols], y_w[:, cols].bitcast(I32))
+        for q in range(4):
+            nc.scalar.dma_start(
+                out_2[0].bitcast(I32)[4 * q : 4 * q + 4, :], y_sc[:].bitcast(I32)[32 * q : 32 * q + 4, :]
+            )

@@ -29,6 +29,7 @@ def tile_picked_pqcdotsend_none_po_kernel(
     with ExitStack() as ctx:
         keep = ctx.enter_context(tc.tile_pool(name="keep", bufs=1))
         reuse = ctx.enter_context(tc.tile_pool(name="reuse", bufs=1))
+        picked = ctx.enter_context(tc.tile_pool(name="picked", bufs=1))
         psum = ctx.enter_context(tc.psum_pool(name="psum", bufs=1))
 
         def load_list(src, name):
@@ -43,23 +44,25 @@ def tile_picked_pqcdotsend_none_po_kernel(
         x_sc = keep.tile([P, T], U8, name="x_sc", align_bytes=64)
         nc.gpsimd.memset(d_sc[:].bitcast(I32), 0)
         nc.vector.memset(x_sc[:].bitcast(I32), 0)
+        dk_sc = keep.tile([P, H], U8, name="dk_sc", align_bytes=64)
+        nc.vector.memset(dk_sc[:].bitcast(I32), 0)
 
         offs_t = load_list(offs, "offs_t")
         x_w = keep.tile([P, T], U32, name="x_w", align_bytes=64)
         nc.sync.dma_start(x_w[:].bitcast(I32), as_words(x_words))
-        nc.scalar.dma_start(d_sc[:].bitcast(I32)[0:P:8, :], d_scales[0].bitcast(I32))
         k1_t = load_list(k1, "k1_t")
         cand_t = load_list(cand, "cand_t")
-        d_w = keep.tile([P, G], U32, name="d_w", align_bytes=64)
+        nc.scalar.dma_start(d_sc[:].bitcast(I32)[0:P:8, :], d_scales[0].bitcast(I32))
+        n2_t = load_list(n2, "n2_t")
+        n1_t = load_list(n1, "n1_t")
+        d_w = picked.tile([P, G], U32, name="d_w", offset=0)
         nc.sync.dma_start(d_w[:].bitcast(I32), as_words(d_words))
         for q in range(4):
             nc.scalar.dma_start(
                 x_sc[:].bitcast(I32)[32 * q : 32 * q + 4, :], x_scales[0].bitcast(I32)[4 * q : 4 * q + 4, :]
             )
         gs_t = keep.tile([P, PACK], F32, name="gs_t")
-        nc.sync.dma_start(gs_t[:], gs.rearrange("(p t) o -> p (t o)", t=PACK))
-        n2_t = load_list(n2, "n2_t")
-        n1_t = load_list(n1, "n1_t")
+        nc.gpsimd.dma_start(gs_t[:], gs.rearrange("(p t) o -> p (t o)", t=PACK))
         n3_t = load_list(n3, "n3_t")
         n4_t = load_list(n4, "n4_t")
         ident = keep.tile([P, P], F32, name="ident")
@@ -75,19 +78,17 @@ def tile_picked_pqcdotsend_none_po_kernel(
         def deal(src, dtype, name):
             tile = keep.tile([P, S], dtype, name=name, align_bytes=64)
             nc.vector.tensor_copy(
-                tile[:].rearrange("p (t m) -> p t m", t=PACK), src[:].rearrange("p (m t) -> p t m", t=PACK)
+                tile[:].rearrange("p (t m) -> p m t", t=PACK), src[:].rearrange("p (m t) -> p m t", t=PACK)
             )
             return tile
 
         xq_w = gather(keep.tile([P, S], U32, name="xq_w", align_bytes=64), x_w, offs_t)
         dk_sc_raw = gather(keep.tile([P, H], U8, name="dk_sc_raw"), d_sc, k1_t)
-        xc_w_raw = gather(keep.tile([P, C], U32, name="xc_w_raw"), x_w, cand_t)
-        dk_sc = deal(dk_sc_raw, U8, "dk_sc")
-        for c in range(1, 4):
-            queue = nc.scalar if c == 2 else nc.sync
-            queue.dma_start(dk_sc[:].bitcast(I32)[c:P:32, :], dk_sc[:].bitcast(I32)[8 * c : P : 32, :])
-        xc_w = deal(xc_w_raw, U32, "xc_w")
-        dk_w_raw = gather(reuse.tile([P, H], U32, name="dk_w_raw", tag="raw"), d_w, k1_t)
+        dk_sc_dealt = deal(dk_sc_raw, U8, "dk_sc_dealt")
+        for c in range(4):
+            queue = (nc.sync, nc.scalar)[c % 2]
+            queue.dma_start(dk_sc[:].bitcast(I32)[c:P:32, :], dk_sc_dealt[:].bitcast(I32)[8 * c : P : 32, :])
+        dk_w_raw = gather(keep.tile([P, H], U32, name="dk_w_raw"), d_w, k1_t)
         xq_sc = gather(keep.tile([P, S], U8, name="xq_sc", align_bytes=64), x_sc, offs_t)
         dk_w = deal(dk_w_raw, U32, "dk_w")
 
@@ -106,7 +107,9 @@ def tile_picked_pqcdotsend_none_po_kernel(
             h_tiles.append(h_t)
             a_tiles.append(a_t)
 
-        xc_sc_raw = gather(reuse.tile([P, C], U8, name="xc_sc_raw", tag="raw"), x_sc, cand_t)
+        xc_w_raw = gather(picked.tile([P, C], U32, name="xc_w_raw", offset=0), x_w, cand_t)
+        xc_sc_raw = gather(picked.tile([P, C], U8, name="xc_sc_raw", offset=4 * C), x_sc, cand_t)
+        xc_w = deal(xc_w_raw, U32, "xc_w")
         xc_sc = deal(xc_sc_raw, U8, "xc_sc")
 
         s_acc = [psum.tile([P, S], F32, name="s_acc%d" % t) for t in range(PACK)]
@@ -123,8 +126,8 @@ def tile_picked_pqcdotsend_none_po_kernel(
             for n, term in enumerate((first, second[:])):
                 for c in range(2):
                     nc.tensor.matmul(
-                        sums[c][:, P * t : P * (t + 1)], lhsT=term[:, P * c : P * (c + 1)], rhs=ident[:],
-                        is_transpose=True, start=(n == 0), stop=(n == 1),
+                        sums[t // 2][:, c, t % 2, :], lhsT=term[:, P * c : P * (c + 1)], rhs=ident[:],
+                        is_transpose=True, start=(t % 2 == 0 and n == 0 and c == 0), stop=(t % 2 == 1 and n == 1 and c == 1),
                     )
 
         def half_lookups(half):
@@ -139,20 +142,21 @@ def tile_picked_pqcdotsend_none_po_kernel(
             return sums
 
         def new_sums(half):
-            return [psum.tile([P, S], F32, name="z_t%d_%d" % (half, c), tag="bank%d" % (2 * half + c)) for c in range(2)]
+            banks = ((0, 1), (2, 1))[half]
+            return [psum.tile([P, 2, 2, P], F32, name="z_t%d_%d" % (half, u), tag="bank%d" % banks[u]) for u in range(2)]
 
         def score(half, sums):
             cols = slice(HALF * half, HALF * (half + 1))
             z_bf = reuse.tile([P, HALF * PACK], BF16, name="z_bf%d" % half, align_bytes=64, tag="z%d" % half)
             z_bf_words = z_bf[:].bitcast(F32).rearrange("p (j u) -> p j u", u=2)
-            for c in range(2):
-                pairs = psum.tile([P, 2, P], F32, name="pairs%d_%d" % (half, c), tag="bank%d" % (2 - 2 * half + c))
-                z_t = keep.tile([P, 2, P, 2], BF16, name="z_t_bf%d_%d" % (half, c))
-                nc.scalar.copy(z_t[:], sums[c][:].rearrange("j (u e p) -> j u p e", u=2, e=2))
-                z_t_words = z_t[:].rearrange("j u p e -> j (u p e)").bitcast(F32)
-                for u in range(2):
-                    nc.tensor.transpose(pairs[:, u, :], z_t_words[:, P * u : P * (u + 1)], ident[:])
-                nc.scalar.copy(z_bf_words[:, P * c : P * (c + 1), :], pairs[:].rearrange("p u j -> p j u"))
+            pairs = psum.tile([P, 2, HALF], F32, name="pairs%d" % half, tag="bank%d" % (2 + half))
+            for u in range(2):
+                z_t = keep.tile([P, 2, P, 2], BF16, name="z_t_bf%d_%d" % (half, u))
+                nc.scalar.copy(z_t[:], sums[u][:].rearrange("j c e p -> j c p e"))
+                z_t_words = z_t[:].rearrange("j c p e -> j (c p e)").bitcast(F32)
+                for c in range(2):
+                    nc.tensor.transpose(pairs[:, u, P * c : P * (c + 1)], z_t_words[:, P * c : P * (c + 1)], ident[:])
+            nc.scalar.copy(z_bf_words, pairs[:].rearrange("p u j -> p j u"))
             z_w = keep.tile([P, HALF], U32, name="z_w%d" % half, align_bytes=64)
             z_sc = keep.tile([P, HALF], U8, name="z_sc%d" % half, align_bytes=64)
             nc.vector.quantize_mx(z_w[:].bitcast(FP8X4), z_sc[:], z_bf[:])
@@ -186,7 +190,7 @@ def tile_picked_pqcdotsend_none_po_kernel(
             )
 
         def finish_on_tensor(t):
-            y_t = psum.tile([P, S], F32, name="y_t%d" % t, tag="bank%d" % (2 + t % 2))
+            y_t = psum.tile([P, S], F32, name="y_t%d" % t, tag="bank%d" % (t % 2))
             for n, term in enumerate((back[t], ds[t])):
                 for c in range(4):
                     cols = slice(P * c, P * (c + 1))
@@ -196,7 +200,7 @@ def tile_picked_pqcdotsend_none_po_kernel(
                     )
             y_t_sb = keep.tile([P, S], F32, name="y_t_sb%d" % t)
             nc.scalar.copy(y_t_sb[:], y_t[:])
-            y_ps = psum.tile([P, S], F32, name="y_ps%d" % t, tag="bank%d" % (t % 2))
+            y_ps = psum.tile([P, S], F32, name="y_ps%d" % t, tag="bank%d" % (2 + t % 2))
             for c in range(4):
                 cols = slice(P * c, P * (c + 1))
                 nc.tensor.transpose(y_ps[:, cols], y_t_sb[:, cols], ident[:])
@@ -208,24 +212,28 @@ def tile_picked_pqcdotsend_none_po_kernel(
         for t in range(PACK - 1):
             scatter(t, 1)
             finish_on_tensor(t)
+        halves = [slice(HALF * half, HALF * (half + 1)) for half in range(2)]
+        y_bf = [keep.tile([P, HALF, PACK], BF16, name="y_bf%d" % half, align_bytes=64) for half in range(2)]
+        for half in range(2):
+            nc.scalar.copy(y_bf[half][:, :, 0:2], y[:, 0:2, halves[half]].rearrange("p t j -> p j t"))
         last = PACK - 1
         nc.vector.tensor_copy(ds[last][:].indirect(n4_t[:]), rl[last][:])
-        nc.vector.scalar_tensor_tensor(y[:, last, :], s_acc[last][:], -0.5 * 0.0625, ds[last][:, 0:S], ALU.mult, ALU.add)
+        for cols in halves:
+            nc.vector.scalar_tensor_tensor(
+                y[:, last, cols], s_acc[last][:, cols], -0.5 * 0.0625, ds[last][:, cols], ALU.mult, ALU.add
+            )
         nc.sync.dma_start(y_rows[:, last, :], y[:, last, :])
 
         y_w = keep.tile([P, S], U32, name="y_w", align_bytes=64)
         y_sc = keep.tile([P, S], U8, name="y_sc", align_bytes=64)
         words_out = as_words(out_1)
+        nc.scalar.copy(y_bf[0][:, :, 2:4], y[:, 2:4, halves[0]].rearrange("p t j -> p j t"))
+        nc.vector.tensor_copy(y_bf[1][:, :, 2:4], y[:, 2:4, halves[1]].rearrange("p t j -> p j t"))
         for half in range(2):
-            cols = slice(HALF * half, HALF * (half + 1))
-            y_bf = keep.tile([P, HALF, PACK], BF16, name="y_bf%d" % half, align_bytes=64)
-            dst = y_bf[:].rearrange("p (c i) t -> p c t i", i=4)
-            src = y[:, :, cols].rearrange("p t (c i) -> p c t i", i=4)
-            if half == 0:
-                nc.vector.tensor_copy(dst, src)
-            else:
-                nc.scalar.copy(dst, src)
-            nc.vector.quantize_mx(y_w[:, cols].bitcast(FP8X4), y_sc[:, cols], y_bf[:].rearrange("p j t -> p (j t)"))
+            cols = halves[half]
+            nc.vector.quantize_mx(
+                y_w[:, cols].bitcast(FP8X4), y_sc[:, cols], y_bf[half][:].rearrange("p j t -> p (j t)")
+            )
             nc.sync.dma_start(words_out[:, cols], y_w[:, cols].bitcast(I32))
         for q in range(4):
             nc.scalar.dma_start(

@@ -198,7 +198,7 @@ def tile_picked_pqcdotsend_none_po_kernel(
                         y_t[:, cols], lhsT=term[:, cols], rhs=ident[:], is_transpose=True,
                         start=(n == 0 and c == 0), stop=(n == 1 and c == 3),
                     )
-            y_t_sb = keep.tile([P, S], F32, name="y_t_sb%d" % t)
+            y_t_sb = reuse.tile([P, S], F32, name="y_t_sb%d" % t, tag="turned%d" % t, align_bytes=64)
             nc.scalar.copy(y_t_sb[:], y_t[:])
             y_ps = psum.tile([P, S], F32, name="y_ps%d" % t, tag="bank%d" % (2 + t % 2))
             for c in range(4):
@@ -213,7 +213,10 @@ def tile_picked_pqcdotsend_none_po_kernel(
             scatter(t, 1)
             finish_on_tensor(t)
         halves = [slice(HALF * half, HALF * (half + 1)) for half in range(2)]
-        y_bf = [keep.tile([P, HALF, PACK], BF16, name="y_bf%d" % half, align_bytes=64) for half in range(2)]
+        y_bf = [
+            reuse.tile([P, HALF, PACK], BF16, name="y_bf%d" % half, tag="turned%d" % (2 * half), align_bytes=64)
+            for half in range(2)
+        ]
         for half in range(2):
             nc.scalar.copy(y_bf[half][:, :, 0:2], y[:, 0:2, halves[half]].rearrange("p t j -> p j t"))
         last = PACK - 1
@@ -222,7 +225,7 @@ def tile_picked_pqcdotsend_none_po_kernel(
             nc.vector.scalar_tensor_tensor(
                 y[:, last, cols], s_acc[last][:, cols], -0.5 * 0.0625, ds[last][:, cols], ALU.mult, ALU.add
             )
-        nc.sync.dma_start(y_rows[:, last, :], y[:, last, :])
+            nc.sync.dma_start(y_rows[:, last, cols], y[:, last, cols])
 
         y_w = keep.tile([P, S], U32, name="y_w", align_bytes=64)
         y_sc = keep.tile([P, S], U8, name="y_sc", align_bytes=64)
@@ -236,6 +239,6 @@ def tile_picked_pqcdotsend_none_po_kernel(
             )
             nc.sync.dma_start(words_out[:, cols], y_w[:, cols].bitcast(I32))
         for q in range(4):
-            nc.scalar.dma_start(
+            (nc.scalar, nc.sync)[q % 2].dma_start(
                 out_2[0].bitcast(I32)[4 * q : 4 * q + 4, :], y_sc[:].bitcast(I32)[32 * q : 32 * q + 4, :]
             )

from contextlib import ExitStack

import concourse.mybir as mybir
from concourse.masks import make_identity

K, T, S, G, H, C = 512, 1024, 512, 2048, 512, 512
FLOPS = 2 * K * H * S + 2 * K * C * S

F32 = mybir.dt.float32
BF16 = mybir.dt.bfloat16
I32 = mybir.dt.int32
U32 = mybir.dt.uint32
U16 = mybir.dt.uint16
U8 = mybir.dt.uint8
FP8X4 = mybir.dt.float8_e4m3fn_x4
ALU = mybir.AluOpType
ACT = mybir.ActivationFunctionType

P = 128
PACK = 4
HALF = S // 2
LIST_COLS = HALF // 16


def tile_picked_pqcdotsend_none_po_kernel(
    tc, x_words, x_scales, d_words, d_scales, gs, offs, k1, n1, n2, n3, cand, n4, out_0, out_1, out_2
):
    nc = tc.nc
    with ExitStack() as ctx:
        keep = ctx.enter_context(tc.tile_pool(name="keep", bufs=1))
        reuse = ctx.enter_context(tc.tile_pool(name="reuse", bufs=1))
        picked = ctx.enter_context(tc.tile_pool(name="picked", bufs=1))
        psum = ctx.enter_context(tc.psum_pool(name="psum", bufs=1))

        def load_list(src, name):
            tile = keep.tile([P, S // 16], U16, name=name)
            nc.sync.dma_start(tile[:], src)
            return tile

        def as_words(src):
            return src[0].rearrange("p n t -> p (n t)").bitcast(I32)

        d_sc = keep.tile([P, G], U8, name="d_sc", align_bytes=64)
        x_sc = keep.tile([P, T], U8, name="x_sc", align_bytes=64)
        nc.gpsimd.memset(d_sc[:].bitcast(I32), 0)
        nc.vector.memset(x_sc[:].bitcast(I32), 0)
        dk_sc = keep.tile([P, H], U8, name="dk_sc", align_bytes=64)
        nc.vector.memset(dk_sc[:].bitcast(I32), 0)

        offs_t = load_list(offs, "offs_t")
        x_w = keep.tile([P, T], U32, name="x_w", align_bytes=64)
        nc.sync.dma_start(x_w[:].bitcast(I32), as_words(x_words))
        k1_t = load_list(k1, "k1_t")
        cand_t = load_list(cand, "cand_t")
        nc.scalar.dma_start(d_sc[:].bitcast(I32)[0:P:8, :], d_scales[0].bitcast(I32))
        n2_t = load_list(n2, "n2_t")
        n1_t = load_list(n1, "n1_t")
        d_w = picked.tile([P, G], U32, name="d_w", offset=0)
        nc.sync.dma_start(d_w[:].bitcast(I32), as_words(d_words))
        for q in range(4):
            nc.scalar.dma_start(
                x_sc[:].bitcast(I32)[32 * q : 32 * q + 4, :], x_scales[0].bitcast(I32)[4 * q : 4 * q + 4, :]
            )
        gs_t = keep.tile([P, PACK], F32, name="gs_t")
        nc.gpsimd.dma_start(gs_t[:], gs.rearrange("(p t) o -> p (t o)", t=PACK))
        n3_t = load_list(n3, "n3_t")
        n4_t = load_list(n4, "n4_t")
        ident = keep.tile([P, P], F32, name="ident")
        make_identity(nc, ident[:])

        gain = keep.tile([P, PACK], F32, name="gain")
        nc.scalar.activation(gain[:], gs_t[:], ACT.Copy, scale=0.75 * 0.0625)

        def gather(tile, src, lst):
            nc.vector.tensor_copy(tile[:], src[:].indirect(lst[:]))
            return tile

        def deal(src, dtype, name):
            tile = keep.tile([P, S], dtype, name=name, align_bytes=64)
            nc.vector.tensor_copy(
                tile[:].rearrange("p (t m) -> p m t", t=PACK), src[:].rearrange("p (m t) -> p m t", t=PACK)
            )
            return tile

        xq_w = gather(keep.tile([P, S], U32, name="xq_w", align_bytes=64), x_w, offs_t)
        dk_sc_raw = gather(keep.tile([P, H], U8, name="dk_sc_raw"), d_sc, k1_t)
        dk_sc_dealt = deal(dk_sc_raw, U8, "dk_sc_dealt")
        for c in range(4):
            queue = (nc.sync, nc.scalar)[c % 2]
            queue.dma_start(dk_sc[:].bitcast(I32)[c:P:32, :], dk_sc_dealt[:].bitcast(I32)[8 * c : P : 32, :])
        dk_w_raw = gather(keep.tile([P, H], U32, name="dk_w_raw"), d_w, k1_t)
        xq_sc = gather(keep.tile([P, S], U8, name="xq_sc", align_bytes=64), x_sc, offs_t)
        dk_w = deal(dk_w_raw, U32, "dk_w")

        h_tiles, a_tiles = [], []
        for t in range(PACK):
            cols = slice(P * t, P * (t + 1))
            acc = psum.tile([P, S], F32, name="h_acc%d" % t, tag="bank%d" % t)
            nc.tensor.matmul_mx(
                out=acc[:], lhsT=dk_w[:, cols].bitcast(FP8X4), lhsT_scale=dk_sc[:, cols],
                rhs=xq_w[:].bitcast(FP8X4), rhs_scale=xq_sc[:], start=True, stop=True,
            )
            h_t = keep.tile([P, S], F32, name="h%d" % t)
            a_t = keep.tile([P, S], F32, name="a%d" % t)
            nc.scalar.activation(h_t[:], acc[:], ACT.Copy, scale=0.0625)
            nc.scalar.activation(a_t[:], acc[:], ACT.Copy, scale=gain[:, t : t + 1])
            h_tiles.append(h_t)
            a_tiles.append(a_t)

        xc_w_raw = gather(picked.tile([P, C], U32, name="xc_w_raw", offset=0), x_w, cand_t)
        xc_sc_raw = gather(picked.tile([P, C], U8, name="xc_sc_raw", offset=4 * C), x_sc, cand_t)
        xc_w = deal(xc_w_raw, U32, "xc_w")
        xc_sc = deal(xc_sc_raw, U8, "xc_sc")

        s_acc = [psum.tile([P, S], F32, name="s_acc%d" % t) for t in range(PACK)]
        rl = [keep.tile([P, S], F32, name="rl%d" % t) for t in range(PACK)]
        back = [keep.tile([P, S], F32, name="back%d" % t) for t in range(PACK - 1)]

        def lookups(half, t, sums, h_n2, first):
            cols = slice(HALF * half, HALF * (half + 1))
            ent = slice(LIST_COLS * half, LIST_COLS * (half + 1))
            second = keep.tile([P, HALF], F32, name="second%d_%d" % (half, t))
            nc.vector.tensor_copy(h_n2, h_tiles[t][:].indirect(n2_t[:, ent]))
            nc.vector.tensor_tensor(first, h_tiles[t][:].indirect(n1_t[:, ent]), a_tiles[t][:, cols], ALU.mult)
            nc.vector.tensor_tensor(second[:], a_tiles[t][:].indirect(n3_t[:, ent]), h_n2, ALU.mult)
            for n, term in enumerate((first, second[:])):
                for c in range(2):
                    nc.tensor.matmul(
                        sums[t // 2][:, c, t % 2, :], lhsT=term[:, P * c : P * (c + 1)], rhs=ident[:],
                        is_transpose=True, start=(t % 2 == 0 and n == 0 and c == 0), stop=(t % 2 == 1 and n == 1 and c == 1),
                    )

        def half_lookups(half):
            sums = new_sums(half)
            first = reuse.tile([P, PACK, HALF], F32, name="first%d" % half, tag="first")
            for pair in range(2):
                tag = ("n2_a", "n2_b", "n2_b", "z0")[2 * half + pair]
                h_n2 = reuse.tile([P, 2, HALF], F32, name="h_n2_%d_%d" % (half, pair), tag=tag, align_bytes=64)
                for e in range(2):
                    t = 2 * pair + e
                    lookups(half, t, sums, h_n2[:, e, :], first[:, t, :])
            return sums

        def new_sums(half):
            banks = ((0, 1), (2, 1))[half]
            return [psum.tile([P, 2, 2, P], F32, name="z_t%d_%d" % (half, u), tag="bank%d" % banks[u]) for u in range(2)]

        def score(half, sums):
            cols = slice(HALF * half, HALF * (half + 1))
            z_bf = reuse.tile([P, HALF * PACK], BF16, name="z_bf%d" % half, align_bytes=64, tag="z%d" % half)
            z_bf_words = z_bf[:].bitcast(F32).rearrange("p (j u) -> p j u", u=2)
            pairs = psum.tile([P, 2, HALF], F32, name="pairs%d" % half, tag="bank%d" % (2 + half))
            for u in range(2):
                z_t = keep.tile([P, 2, P, 2], BF16, name="z_t_bf%d_%d" % (half, u))
                nc.scalar.copy(z_t[:], sums[u][:].rearrange("j c e p -> j c p e"))
                z_t_words = z_t[:].rearrange("j c p e -> j (c p e)").bitcast(F32)
                for c in range(2):
                    nc.tensor.transpose(pairs[:, u, P * c : P * (c + 1)], z_t_words[:, P * c : P * (c + 1)], ident[:])
            nc.scalar.copy(z_bf_words, pairs[:].rearrange("p u j -> p j u"))
            z_w = keep.tile([P, HALF], U32, name="z_w%d" % half, align_bytes=64)
            z_sc = keep.tile([P, HALF], U8, name="z_sc%d" % half, align_bytes=64)
            nc.vector.quantize_mx(z_w[:].bitcast(FP8X4), z_sc[:], z_bf[:])
            for t in range(PACK):
                rows = slice(P * t, P * (t + 1))
                nc.tensor.matmul_mx(
                    out=s_acc[t][:, cols], lhsT=xc_w[:, rows].bitcast(FP8X4), lhsT_scale=xc_sc[:, rows],
                    rhs=z_w[:].bitcast(FP8X4), rhs_scale=z_sc[:], start=True, stop=True,
                )
                nc.scalar.activation(rl[t][:, cols], s_acc[t][:, cols], ACT.Relu, scale=0.0625)
            for t in range(PACK - 1):
                nc.scalar.activation(back[t][:, cols], s_acc[t][:, cols], ACT.Copy, scale=-0.5 * 0.0625)
            return z_w

        zw0 = score(0, half_lookups(0))
        zw1 = score(1, half_lookups(1))

        ds = [
            keep.tile([P, S], F32, name="ds0"),
            keep.tile([P, S], F32, name="ds1"),
            reuse.tile([P, S], F32, name="ds2", tag="z1", align_bytes=64),
            keep.tile([P, 2 * S], F32, name="ds3"),
        ]
        y = keep.tile([P, PACK, S], F32, name="y")
        y_rows = out_0.rearrange("(p t) j -> p t j", t=PACK)

        def scatter(t, half):
            nc.vector.tensor_copy(
                ds[t][:].indirect(n4_t[:, LIST_COLS * half : LIST_COLS * (half + 1)]),
                rl[t][:, HALF * half : HALF * (half + 1)],
            )

        def finish_on_tensor(t):
            y_t = psum.tile([P, S], F32, name="y_t%d" % t, tag="bank%d" % (t % 2))
            for n, term in enumerate((back[t], ds[t])):
                for c in range(4):
                    cols = slice(P * c, P * (c + 1))
                    nc.tensor.matmul(
                        y_t[:, cols], lhsT=term[:, cols], rhs=ident[:], is_transpose=True,
                        start=(n == 0 and c == 0), stop=(n == 1 and c == 3),
                    )
            y_t_sb = reuse.tile([P, S], F32, name="y_t_sb%d" % t, tag="turned%d" % t, align_bytes=64)
            nc.scalar.copy(y_t_sb[:], y_t[:])
            y_ps = psum.tile([P, S], F32, name="y_ps%d" % t, tag="bank%d" % (2 + t % 2))
            for c in range(4):
                cols = slice(P * c, P * (c + 1))
                nc.tensor.transpose(y_ps[:, cols], y_t_sb[:, cols], ident[:])
            nc.scalar.copy(y[:, t, :], y_ps[:])
            nc.sync.dma_start(y_rows[:, t, :], y[:, t, :])

        for t in range(PACK - 1):
            scatter(t, 0)
        for t in range(PACK - 1):
            scatter(t, 1)
            finish_on_tensor(t)
        halves = [slice(HALF * half, HALF * (half + 1)) for half in range(2)]
        y_bf = [
            reuse.tile([P, HALF, PACK], BF16, name="y_bf%d" % half, tag="turned%d" % (2 * half), align_bytes=64)
            for half in range(2)
        ]
        for half in range(2):
            nc.scalar.copy(y_bf[half][:, :, 0:2], y[:, 0:2, halves[half]].rearrange("p t j -> p j t"))
        last = PACK - 1
        nc.vector.tensor_copy(ds[last][:].indirect(n4_t[:]), rl[last][:])
        for cols in halves:
            nc.vector.scalar_tensor_tensor(
                y[:, last, cols], s_acc[last][:, cols], -0.5 * 0.0625, ds[last][:, cols], ALU.mult, ALU.add
            )
            nc.sync.dma_start(y_rows[:, last, cols], y[:, last, cols])

        y_w = keep.tile([P, S], U32, name="y_w", align_bytes=64)
        y_sc = keep.tile([P, S], U8, name="y_sc", align_bytes=64)
        words_out = as_words(out_1)
        nc.scalar.copy(y_bf[0][:, :, 2:4], y[:, 2:4, halves[0]].rearrange("p t j -> p j t"))
        nc.vector.tensor_copy(y_bf[1][:, :, 2:4], y[:, 2:4, halves[1]].rearrange("p t j -> p j t"))
        for half in range(2):
            cols = halves[half]
            nc.vector.quantize_mx(
                y_w[:, cols].bitcast(FP8X4), y_sc[:, cols], y_bf[half][:].rearrange("p j t -> p (j t)")
            )
            nc.sync.dma_start(words_out[:, cols], y_w[:, cols].bitcast(I32))
        for q in range(4):
            (nc.scalar, nc.sync)[q % 2].dma_start(
                out_2[0].bitcast(I32)[4 * q : 4 * q + 4, :], y_sc[:].bitcast(I32)[32 * q : 32 * q + 4, :]
            )
